import numpy as np
import ml_dtypes


def mxq(x, axis, fmt="e4m3"):
    dtype, down = {"e4m3": (ml_dtypes.float8_e4m3fn, 7), "e5m2": (ml_dtypes.float8_e5m2, 14)}[fmt]
    v = np.moveaxis(np.asarray(x, np.float32).astype(ml_dtypes.bfloat16).astype(np.float64), axis, -1)
    blocks = v.reshape(v.shape[:-1] + (-1, 32))
    amax = np.abs(blocks).max(-1, keepdims=True)
    byte = np.maximum(np.where(amax > 0, np.frexp(amax)[1] - 1 + 127, 0) - down, 1)
    scale = np.exp2(byte - 127.0)
    codes = (blocks / scale).astype(np.float32).astype(dtype).astype(np.float64)
    return np.moveaxis((codes * scale).reshape(v.shape), -1, axis)


WIDE = False


def mx_kscale(k, group=512):
    if not WIDE:
        return np.ones(k)
    levels = np.array([10, -10, 5, -5, 0])
    if group != 512:
        return np.exp2(np.random.permutation(np.resize(levels, k // group))).repeat(group)
    if k % 512:
        return np.exp2(np.random.permutation(np.resize(levels, k // 32))).repeat(32)
    a = np.empty((k // 512, 16))
    for p in range(k // 512):
        a[p, :8] = np.random.permutation(np.resize(levels, 8))
        for g in range(8):
            far = levels[np.abs(levels - a[p, g]) >= 10]
            a[p, g + 8] = far[np.random.randint(len(far))]
    return np.exp2(a.ravel()).repeat(32)


def f64(x):
    return np.asarray(x).astype(np.float64)


def gelu(v):
    return 0.5 * v * (1.0 + np.tanh(0.7978845608028654 * (v + 0.044715 * v ** 3)))


G, D, M, N = 2, 256, 256, 512


def setup_inputs():
    n = np.random.standard_normal
    s = mx_kscale(D, 0)[:, None]
    return {
        "x": (n((G, D, N)) * s).astype(np.float32),
        "w": (n((G, D, M)) / np.sqrt(D) / s).astype(np.float32),
        "u": (n((G, D, M)) / np.sqrt(D) / s).astype(np.float32),
    }


def reference(x, w, u):
    xq = mxq(f64(x), 1, "e4m3")
    h = mxq(f64(w), 1, "e4m3").transpose(0, 2, 1) @ xq
    g = mxq(f64(u), 1, "e4m3").transpose(0, 2, 1) @ xq
    y = gelu(h) * g
    return y

@@ -1,0 +1,158 @@
+from contextlib import ExitStack
+
+import concourse.mybir as mybir
+
+G, D, M, N = 2, 256, 256, 512
+FLOPS = 2 * 2 * G * D * M * N
+
+F32 = mybir.dt.float32
+BF16 = mybir.dt.bfloat16
+U32 = mybir.dt.uint32
+U8 = mybir.dt.uint8
+FP8X4 = mybir.dt.float8_e4m3fn_x4
+GELU = mybir.ActivationFunctionType.Gelu_apprx_tanh
+MULT = mybir.AluOpType.mult
+
+P = 128
+PACK = 4
+ROWS = D // PACK
+T = 128
+RUN = 4
+
+
+def tile_rows_gglu_gelu_kernel(tc, x, w, u, out):
+    nc = tc.nc
+    with ExitStack() as ctx:
+        sb = ctx.enter_context(tc.tile_pool(name="sb", bufs=1))
+        ps = ctx.enter_context(tc.psum_pool(name="ps", bufs=1))
+        ctx.enter_context(tc.manual_schedule())
+
+        rows = "g (p j) c -> (g p) j c"
+        x_rows = x.rearrange(rows, j=PACK)
+        w_rows = w.rearrange(rows, j=PACK)
+        u_rows = u.rearrange(rows, j=PACK)
+        out_rows = out.rearrange("g (t p) n -> p (g t) n", p=P)
+
+        def operand(name, width):
+            return {
+                "grouped": sb.tile([P, width, PACK], BF16, name=name + "_grouped", align_bytes=64),
+                "codes": sb.tile([P, width], U32, name=name + "_codes", align_bytes=64),
+                "scales": sb.tile([P, width], U8, name=name + "_scales", align_bytes=64),
+            }
+
+        def load(name, src, c0, c1, eng=nc.sync):
+            raw = sb.tile([P, PACK, c1 - c0], F32, name=name + "_raw", align_bytes=64)
+            eng.dma_start(out=raw[:], in_=src[:, :, c0:c1])
+            return raw
+
+        def interleave(copy, op, o0, raw, r0, width):
+            copy(
+                out=op["grouped"][:, o0 : o0 + width, :].rearrange("p (c i) j -> p c j i", i=RUN),
+                in_=raw[:, :, r0 : r0 + width].rearrange("p j (c i) -> p c j i", i=RUN),
+            )
+
+        def quantize(op, c0, c1):
+            nc.vector.quantize_mx(
+                out=op["codes"][:, c0:c1].bitcast(FP8X4),
+                scales=op["scales"][:, c0:c1],
+                in_=op["grouped"][:, c0:c1, :].rearrange("p c j -> p (c j)"),
+            )
+
+        def product(dst, weights, t, xop, c0, g):
+            part = slice(g * ROWS, (g + 1) * ROWS)
+            nc.tensor.matmul_mx(
+                out=dst,
+                lhsT=weights["codes"][part, t * T : (t + 1) * T].bitcast(FP8X4),
+                lhsT_scale=weights["scales"][part, t * T : (t + 1) * T],
+                rhs=xop["codes"][part, c0 : c0 + T].bitcast(FP8X4),
+                rhs_scale=xop["scales"][part, c0 : c0 + T],
+                start=True,
+                stop=True,
+            )
+
+        def products(bank, weights, xop, c0, width):
+            for n0 in range(0, width, T):
+                for t in range(2):
+                    for g in range(G):
+                        o = t * width + n0
+                        product(banks[g][bank][:, o : o + T], weights, t, xop, c0 + n0, g)
+
+        def gelu(g, bank, act, width):
+            nc.scalar.activation(out=act[:, g, :], in_=banks[g][bank][:, : 2 * width], func=GELU)
+
+        def gate(g, bank, act, res, width):
+            nc.vector.tensor_tensor(out=res[:, g, :], in0=banks[g][bank][:, : 2 * width], in1=act[:, g, :], op=MULT)
+
+        def store(res, c0, width, g0, g1, eng=nc.sync):
+            eng.dma_start(
+                out=out_rows[:, 2 * g0 : 2 * g1, c0 : c0 + width],
+                in_=res[:, g0:g1, :].rearrange("p g (t n) -> p (g t) n", t=2),
+            )
+
+        def result(name, width):
+            act = sb.tile([P, G, 2 * width], F32, name=name + "_act", align_bytes=64)
+            res = sb.tile([P, G, 2 * width], F32, name=name + "_res", align_bytes=64)
+            return act, res
+
+        banks = [[ps.tile([P, 512], F32, name="bank%d_%d" % (g, b)) for b in range(4)] for g in range(G)]
+        vcopy = nc.vector.tensor_copy
+        scopy = nc.scalar.copy
+
+        warm_in = sb.tile([P, 8], F32, name="warm_in")
+        warm_out = sb.tile([P, 8], F32, name="warm_out")
+
+        w_raw = load("w", w_rows, 0, M)
+        xa_raw = load("xa", x_rows, 0, 256)
+        u_raw = load("u", u_rows, 0, M)
+        xb_raw = load("xb", x_rows, 256, 384)
+        xc_raw = load("xc", x_rows, 384, 512)
+
+        nc.vector.memset(warm_in[:], 0.0)
+        nc.scalar.activation(out=warm_out[:], in_=warm_in[:], func=GELU)
+
+        wq, uq = operand("w", M), operand("u", M)
+        xa, xb, xc = operand("xa", 256), operand("xb", T), operand("xc", T)
+        act_a, res_a = result("a", 256)
+        act_b, res_b = result("b", T)
+        act_c, res_c = result("c", T)
+
+        interleave(vcopy, wq, 0, w_raw, 0, 160)
+        interleave(scopy, wq, 160, w_raw, 160, 96)
+        quantize(wq, 0, M)
+
+        interleave(vcopy, xa, 0, xa_raw, 0, 160)
+        interleave(scopy, xa, 160, xa_raw, 160, 96)
+        quantize(xa, 0, 256)
+        products(0, wq, xa, 0, 256)
+
+        interleave(vcopy, uq, 0, u_raw, 0, 160)
+        interleave(scopy, uq, 160, u_raw, 160, 96)
+        quantize(uq, 0, M)
+        gelu(0, 0, act_a, 256)
+        gelu(1, 0, act_a, 256)
+        products(1, uq, xa, 0, 256)
+
+        interleave(vcopy, xb, 0, xb_raw, 0, T)
+        quantize(xb, 0, T)
+        products(2, wq, xb, 0, T)
+        gate(0, 1, act_a, res_a, 256)
+        store(res_a, 0, 256, 0, 1)
+        products(0, uq, xb, 0, T)
+
+        interleave(scopy, xc, 0, xc_raw, 0, T)
+        quantize(xc, 0, T)
+        products(3, wq, xc, 0, T)
+        gelu(0, 2, act_b, T)
+        gelu(1, 2, act_b, T)
+        gate(1, 1, act_a, res_a, 256)
+        store(res_a, 0, 256, 1, 2)
+        products(2, uq, xc, 0, T)
+        gate(0, 0, act_b, res_b, T)
+        gate(1, 0, act_b, res_b, T)
+        store(res_b, 256, T, 0, 2)
+        gelu(0, 3, act_c, T)
+        gelu(1, 3, act_c, T)
+        gate(0, 2, act_c, res_c, T)
+        store(res_c, 384, T, 0, 1)
+        gate(1, 2, act_c, res_c, T)
+        store(res_c, 384, T, 1, 2)

@@ -31,7 +31,6 @@ def tile_rows_gglu_gelu_kernel(tc, x, w, u, out):
         x_rows = x.rearrange(rows, j=PACK)
         w_rows = w.rearrange(rows, j=PACK)
         u_rows = u.rearrange(rows, j=PACK)
-        out_rows = out.rearrange("g (t p) n -> p (g t) n", p=P)
 
         def operand(name, width):
             return {
@@ -58,101 +57,104 @@ def tile_rows_gglu_gelu_kernel(tc, x, w, u, out):
                 in_=op["grouped"][:, c0:c1, :].rearrange("p c j -> p (c j)"),
             )
 
-        def product(dst, weights, t, xop, c0, g):
+        def product(bank, weights, xop, g):
             part = slice(g * ROWS, (g + 1) * ROWS)
             nc.tensor.matmul_mx(
-                out=dst,
-                lhsT=weights["codes"][part, t * T : (t + 1) * T].bitcast(FP8X4),
-                lhsT_scale=weights["scales"][part, t * T : (t + 1) * T],
-                rhs=xop["codes"][part, c0 : c0 + T].bitcast(FP8X4),
-                rhs_scale=xop["scales"][part, c0 : c0 + T],
+                out=banks[g][bank][:],
+                lhsT=weights["codes"][part, 0:T].bitcast(FP8X4),
+                lhsT_scale=weights["scales"][part, 0:T],
+                rhs=xop["codes"][part, :].bitcast(FP8X4),
+                rhs_scale=xop["scales"][part, :],
                 start=True,
                 stop=True,
             )
 
-        def products(bank, weights, xop, c0, width):
-            for n0 in range(0, width, T):
-                for t in range(2):
-                    for g in range(G):
-                        o = t * width + n0
-                        product(banks[g][bank][:, o : o + T], weights, t, xop, c0 + n0, g)
+        def products(bank, weights, xop):
+            for g in range(G):
+                product(bank, weights, xop, g)
 
-        def gelu(g, bank, act, width):
-            nc.scalar.activation(out=act[:, g, :], in_=banks[g][bank][:, : 2 * width], func=GELU)
+        def gelu(g, t):
+            nc.scalar.activation(out=act[g][t][:], in_=banks[g][2 * t][:], func=GELU)
 
-        def gate(g, bank, act, res, width):
-            nc.vector.tensor_tensor(out=res[:, g, :], in0=banks[g][bank][:, : 2 * width], in1=act[:, g, :], op=MULT)
+        def gate(g, t, n0=0, n1=N, eng=nc.sync):
+            res = sb.tile([P, n1 - n0], F32, name="res%d_%d_%d" % (g, t, n0), align_bytes=64)
+            nc.vector.tensor_tensor(out=res[:], in0=banks[g][2 * t + 1][:, n0:n1], in1=act[g][t][:, n0:n1], op=MULT)
+            eng.dma_start(out=out[g, t * T : (t + 1) * T, n0:n1], in_=res[:])
 
-        def store(res, c0, width, g0, g1, eng=nc.sync):
-            eng.dma_start(
-                out=out_rows[:, 2 * g0 : 2 * g1, c0 : c0 + width],
-                in_=res[:, g0:g1, :].rearrange("p g (t n) -> p (g t) n", t=2),
+        act = [[sb.tile([P, N], F32, name="act%d_%d" % (g, t), align_bytes=64) for t in range(2)] for g in range(G)]
+        owned = [[ps.tile([P, N], F32, name="bank%d_%d" % (g, b)) for b in range(3 + g)] for g in range(G)]
+        banks = [owned[0] + owned[0][:1], owned[1]]
+        idle_bank = ps.tile([P, N], F32, name="idle_bank")
+
+        def idle_pass(weights, moving):
+            nc.tensor.matmul_mx(
+                out=idle_bank[:],
+                lhsT=weights["codes"][:, 0:T].bitcast(FP8X4),
+                lhsT_scale=weights["scales"][:, 0:T],
+                rhs=moving["codes"][:].bitcast(FP8X4),
+                rhs_scale=moving["scales"][:],
+                start=True,
+                stop=True,
             )
 
-        def result(name, width):
-            act = sb.tile([P, G, 2 * width], F32, name=name + "_act", align_bytes=64)
-            res = sb.tile([P, G, 2 * width], F32, name=name + "_res", align_bytes=64)
-            return act, res
-
-        banks = [[ps.tile([P, 512], F32, name="bank%d_%d" % (g, b)) for b in range(4)] for g in range(G)]
         vcopy = nc.vector.tensor_copy
         scopy = nc.scalar.copy
 
         warm_in = sb.tile([P, 8], F32, name="warm_in")
         warm_out = sb.tile([P, 8], F32, name="warm_out")
 
-        w_raw = load("w", w_rows, 0, M)
         xa_raw = load("xa", x_rows, 0, 256)
-        u_raw = load("u", u_rows, 0, M)
-        xb_raw = load("xb", x_rows, 256, 384)
-        xc_raw = load("xc", x_rows, 384, 512)
+        xb_raw = load("xb", x_rows, 256, 512)
+        w0_raw = load("w0", w_rows, 0, T)
+        u0_raw = load("u0", u_rows, 0, T)
+        w1_raw = load("w1", w_rows, T, M)
+        u1_raw = load("u1", u_rows, T, M)
 
         nc.vector.memset(warm_in[:], 0.0)
         nc.scalar.activation(out=warm_out[:], in_=warm_in[:], func=GELU)
 
-        wq, uq = operand("w", M), operand("u", M)
-        xa, xb, xc = operand("xa", 256), operand("xb", T), operand("xc", T)
-        act_a, res_a = result("a", 256)
-        act_b, res_b = result("b", T)
-        act_c, res_c = result("c", T)
+        zeros = operand("zeros", N)
+        nc.vector.memset(zeros["grouped"][:, 0:T, :], 0.0)
+        for c0 in range(0, N, T):
+            nc.vector.quantize_mx(
+                out=zeros["codes"][:, c0 : c0 + T].bitcast(FP8X4),
+                scales=zeros["scales"][:, c0 : c0 + T],
+                in_=zeros["grouped"][:, 0:T, :].rearrange("p c j -> p (c j)"),
+            )
+        for i in range(7):
+            idle_pass(zeros, zeros)
+        xq = operand("x", N)
+        w0, u0, w1, u1 = operand("w0", T), operand("u0", T), operand("w1", T), operand("u1", T)
 
-        interleave(vcopy, wq, 0, w_raw, 0, 160)
-        interleave(scopy, wq, 160, w_raw, 160, 96)
-        quantize(wq, 0, M)
+        interleave(vcopy, xq, 0, xa_raw, 0, 160)
+        interleave(scopy, xq, 160, xa_raw, 160, 96)
+        quantize(xq, 0, 256)
+        for i in range(2):
+            idle_pass(xq, zeros)
+        interleave(vcopy, xq, 256, xb_raw, 0, 160)
+        interleave(scopy, xq, 416, xb_raw, 160, 96)
+        quantize(xq, 256, 512)
 
-        interleave(vcopy, xa, 0, xa_raw, 0, 160)
-        interleave(scopy, xa, 160, xa_raw, 160, 96)
-        quantize(xa, 0, 256)
-        products(0, wq, xa, 0, 256)
-
-        interleave(vcopy, uq, 0, u_raw, 0, 160)
-        interleave(scopy, uq, 160, u_raw, 160, 96)
-        quantize(uq, 0, M)
-        gelu(0, 0, act_a, 256)
-        gelu(1, 0, act_a, 256)
-        products(1, uq, xa, 0, 256)
-
-        interleave(vcopy, xb, 0, xb_raw, 0, T)
-        quantize(xb, 0, T)
-        products(2, wq, xb, 0, T)
-        gate(0, 1, act_a, res_a, 256)
-        store(res_a, 0, 256, 0, 1)
-        products(0, uq, xb, 0, T)
-
-        interleave(scopy, xc, 0, xc_raw, 0, T)
-        quantize(xc, 0, T)
-        products(3, wq, xc, 0, T)
-        gelu(0, 2, act_b, T)
-        gelu(1, 2, act_b, T)
-        gate(1, 1, act_a, res_a, 256)
-        store(res_a, 0, 256, 1, 2)
-        products(2, uq, xc, 0, T)
-        gate(0, 0, act_b, res_b, T)
-        gate(1, 0, act_b, res_b, T)
-        store(res_b, 256, T, 0, 2)
-        gelu(0, 3, act_c, T)
-        gelu(1, 3, act_c, T)
-        gate(0, 2, act_c, res_c, T)
-        store(res_c, 384, T, 0, 1)
-        gate(1, 2, act_c, res_c, T)
-        store(res_c, 384, T, 1, 2)
+        interleave(vcopy, w0, 0, w0_raw, 0, 80)
+        interleave(scopy, w0, 80, w0_raw, 80, 48)
+        quantize(w0, 0, T)
+        products(0, w0, xq)
+        interleave(vcopy, u0, 0, u0_raw, 0, 80)
+        interleave(scopy, u0, 80, u0_raw, 80, 48)
+        quantize(u0, 0, T)
+        products(1, u0, xq)
+        interleave(vcopy, w1, 0, w1_raw, 0, 80)
+        interleave(scopy, w1, 80, w1_raw, 80, 48)
+        quantize(w1, 0, T)
+        products(2, w1, xq)
+        interleave(vcopy, u1, 0, u1_raw, 0, T)
+        quantize(u1, 0, T)
+        gelu(0, 0)
+        products(3, u1, xq)
+        gate(0, 0)
+        gelu(1, 0)
+        gate(1, 0)
+        gelu(0, 1)
+        gate(0, 1)
+        gelu(1, 1)
+        gate(1, 1)

@@ -57,21 +57,21 @@ def tile_rows_gglu_gelu_kernel(tc, x, w, u, out):
                 in_=op["grouped"][:, c0:c1, :].rearrange("p c j -> p (c j)"),
             )
 
-        def product(bank, weights, xop, g):
+        def product(bank, weights, xop, g, c0=0):
             part = slice(g * ROWS, (g + 1) * ROWS)
             nc.tensor.matmul_mx(
                 out=banks[g][bank][:],
-                lhsT=weights["codes"][part, 0:T].bitcast(FP8X4),
-                lhsT_scale=weights["scales"][part, 0:T],
+                lhsT=weights["codes"][part, c0 : c0 + T].bitcast(FP8X4),
+                lhsT_scale=weights["scales"][part, c0 : c0 + T],
                 rhs=xop["codes"][part, :].bitcast(FP8X4),
                 rhs_scale=xop["scales"][part, :],
                 start=True,
                 stop=True,
             )
 
-        def products(bank, weights, xop):
+        def products(bank, weights, xop, c0=0):
             for g in range(G):
-                product(bank, weights, xop, g)
+                product(bank, weights, xop, g, c0)
 
         def gelu(g, t):
             nc.scalar.activation(out=act[g][t][:], in_=banks[g][2 * t][:], func=GELU)
@@ -103,16 +103,13 @@ def tile_rows_gglu_gelu_kernel(tc, x, w, u, out):
         warm_in = sb.tile([P, 8], F32, name="warm_in")
         warm_out = sb.tile([P, 8], F32, name="warm_out")
 
-        xa_raw = load("xa", x_rows, 0, 256)
-        xb_raw = load("xb", x_rows, 256, 512)
-        w0_raw = load("w0", w_rows, 0, T)
+        x_raw = load("x", x_rows, 0, N)
+        w_raw = load("w", w_rows, 0, M)
         u0_raw = load("u0", u_rows, 0, T)
-        w1_raw = load("w1", w_rows, T, M)
         u1_raw = load("u1", u_rows, T, M)
 
         nc.vector.memset(warm_in[:], 0.0)
         nc.scalar.activation(out=warm_out[:], in_=warm_in[:], func=GELU)
-
         zeros = operand("zeros", N)
         nc.vector.memset(zeros["grouped"][:, 0:T, :], 0.0)
         for c0 in range(0, N, T):
@@ -121,36 +118,33 @@ def tile_rows_gglu_gelu_kernel(tc, x, w, u, out):
                 scales=zeros["scales"][:, c0 : c0 + T],
                 in_=zeros["grouped"][:, 0:T, :].rearrange("p c j -> p (c j)"),
             )
-        for i in range(7):
+        for i in range(8):
             idle_pass(zeros, zeros)
-        xq = operand("x", N)
-        w0, u0, w1, u1 = operand("w0", T), operand("u0", T), operand("w1", T), operand("u1", T)
 
-        interleave(vcopy, xq, 0, xa_raw, 0, 160)
-        interleave(scopy, xq, 160, xa_raw, 160, 96)
+        xq = operand("x", N)
+        wq, uq = operand("w", M), operand("u", M)
+
+        interleave(vcopy, xq, 0, x_raw, 0, 256)
+        interleave(scopy, xq, 320, x_raw, 320, 192)
+        interleave(vcopy, xq, 256, x_raw, 256, 64)
         quantize(xq, 0, 256)
         for i in range(2):
             idle_pass(xq, zeros)
-        interleave(vcopy, xq, 256, xb_raw, 0, 160)
-        interleave(scopy, xq, 416, xb_raw, 160, 96)
-        quantize(xq, 256, 512)
-
-        interleave(vcopy, w0, 0, w0_raw, 0, 80)
-        interleave(scopy, w0, 80, w0_raw, 80, 48)
-        quantize(w0, 0, T)
-        products(0, w0, xq)
-        interleave(vcopy, u0, 0, u0_raw, 0, 80)
-        interleave(scopy, u0, 80, u0_raw, 80, 48)
-        quantize(u0, 0, T)
-        products(1, u0, xq)
-        interleave(vcopy, w1, 0, w1_raw, 0, 80)
-        interleave(scopy, w1, 80, w1_raw, 80, 48)
-        quantize(w1, 0, T)
-        products(2, w1, xq)
-        interleave(vcopy, u1, 0, u1_raw, 0, T)
-        quantize(u1, 0, T)
+        quantize(xq, 256, N)
+        interleave(vcopy, wq, 0, w_raw, 0, 48)
+        interleave(scopy, wq, 48, w_raw, 48, 80)
+        interleave(scopy, wq, 128, w_raw, 128, 128)
+        quantize(wq, 0, T)
+        products(0, wq, xq, 0)
+        interleave(vcopy, uq, 0, u0_raw, 0, T)
+        quantize(wq, T, M)
+        quantize(uq, 0, T)
+        products(1, uq, xq, 0)
+        products(2, wq, xq, T)
+        interleave(vcopy, uq, T, u1_raw, 0, T)
         gelu(0, 0)
-        products(3, u1, xq)
+        quantize(uq, T, M)
+        products(3, uq, xq, T)
         gate(0, 0)
         gelu(1, 0)
         gate(1, 0)

from contextlib import ExitStack

import concourse.mybir as mybir

G, D, M, N = 2, 256, 256, 512
FLOPS = 2 * 2 * G * D * M * N

F32 = mybir.dt.float32
BF16 = mybir.dt.bfloat16
U32 = mybir.dt.uint32
U8 = mybir.dt.uint8
FP8X4 = mybir.dt.float8_e4m3fn_x4
GELU = mybir.ActivationFunctionType.Gelu_apprx_tanh
MULT = mybir.AluOpType.mult

P = 128
PACK = 4
ROWS = D // PACK
T = 128
RUN = 4


def tile_rows_gglu_gelu_kernel(tc, x, w, u, out):
    nc = tc.nc
    with ExitStack() as ctx:
        sb = ctx.enter_context(tc.tile_pool(name="sb", bufs=1))
        ps = ctx.enter_context(tc.psum_pool(name="ps", bufs=1))
        ctx.enter_context(tc.manual_schedule())

        rows = "g (p j) c -> (g p) j c"
        x_rows = x.rearrange(rows, j=PACK)
        w_rows = w.rearrange(rows, j=PACK)
        u_rows = u.rearrange(rows, j=PACK)

        def operand(name, width):
            return {
                "grouped": sb.tile([P, width, PACK], BF16, name=name + "_grouped", align_bytes=64),
                "codes": sb.tile([P, width], U32, name=name + "_codes", align_bytes=64),
                "scales": sb.tile([P, width], U8, name=name + "_scales", align_bytes=64),
            }

        def load(name, src, c0, c1, eng=nc.sync):
            raw = sb.tile([P, PACK, c1 - c0], F32, name=name + "_raw", align_bytes=64)
            eng.dma_start(out=raw[:], in_=src[:, :, c0:c1])
            return raw

        def interleave(copy, op, o0, raw, r0, width):
            copy(
                out=op["grouped"][:, o0 : o0 + width, :].rearrange("p (c i) j -> p c j i", i=RUN),
                in_=raw[:, :, r0 : r0 + width].rearrange("p j (c i) -> p c j i", i=RUN),
            )

        def quantize(op, c0, c1):
            nc.vector.quantize_mx(
                out=op["codes"][:, c0:c1].bitcast(FP8X4),
                scales=op["scales"][:, c0:c1],
                in_=op["grouped"][:, c0:c1, :].rearrange("p c j -> p (c j)"),
            )

        def product(bank, weights, xop, g, c0=0):
            part = slice(g * ROWS, (g + 1) * ROWS)
            nc.tensor.matmul_mx(
                out=banks[g][bank][:],
                lhsT=weights["codes"][part, c0 : c0 + T].bitcast(FP8X4),
                lhsT_scale=weights["scales"][part, c0 : c0 + T],
                rhs=xop["codes"][part, :].bitcast(FP8X4),
                rhs_scale=xop["scales"][part, :],
                start=True,
                stop=True,
            )

        def products(bank, weights, xop, c0=0):
            for g in range(G):
                product(bank, weights, xop, g, c0)

        def gelu(g, t):
            nc.scalar.activation(out=act[g][t][:], in_=banks[g][2 * t][:], func=GELU)

        def gate(g, t, n0=0, n1=N, eng=nc.sync):
            res = sb.tile([P, n1 - n0], F32, name="res%d_%d_%d" % (g, t, n0), align_bytes=64)
            nc.vector.tensor_tensor(out=res[:], in0=banks[g][2 * t + 1][:, n0:n1], in1=act[g][t][:, n0:n1], op=MULT)
            eng.dma_start(out=out[g, t * T : (t + 1) * T, n0:n1], in_=res[:])

        act = [[sb.tile([P, N], F32, name="act%d_%d" % (g, t), align_bytes=64) for t in range(2)] for g in range(G)]
        owned = [[ps.tile([P, N], F32, name="bank%d_%d" % (g, b)) for b in range(3 + g)] for g in range(G)]
        banks = [owned[0] + owned[0][:1], owned[1]]
        idle_bank = ps.tile([P, N], F32, name="idle_bank")

        def idle_pass(weights, moving):
            nc.tensor.matmul_mx(
                out=idle_bank[:],
                lhsT=weights["codes"][:, 0:T].bitcast(FP8X4),
                lhsT_scale=weights["scales"][:, 0:T],
                rhs=moving["codes"][:].bitcast(FP8X4),
                rhs_scale=moving["scales"][:],
                start=True,
                stop=True,
            )

        vcopy = nc.vector.tensor_copy
        scopy = nc.scalar.copy

        warm_in = sb.tile([P, 8], F32, name="warm_in")
        warm_out = sb.tile([P, 8], F32, name="warm_out")

        x_raw = load("x", x_rows, 0, N)
        w_raw = load("w", w_rows, 0, M)
        u0_raw = load("u0", u_rows, 0, T)
        u1_raw = load("u1", u_rows, T, M)

        nc.vector.memset(warm_in[:], 0.0)
        nc.scalar.activation(out=warm_out[:], in_=warm_in[:], func=GELU)
        zeros = operand("zeros", N)
        nc.vector.memset(zeros["grouped"][:, 0:T, :], 0.0)
        for c0 in range(0, N, T):
            nc.vector.quantize_mx(
                out=zeros["codes"][:, c0 : c0 + T].bitcast(FP8X4),
                scales=zeros["scales"][:, c0 : c0 + T],
                in_=zeros["grouped"][:, 0:T, :].rearrange("p c j -> p (c j)"),
            )
        for i in range(8):
            idle_pass(zeros, zeros)

        xq = operand("x", N)
        wq, uq = operand("w", M), operand("u", M)

        interleave(vcopy, xq, 0, x_raw, 0, 256)
        interleave(scopy, xq, 320, x_raw, 320, 192)
        interleave(vcopy, xq, 256, x_raw, 256, 64)
        quantize(xq, 0, 256)
        for i in range(2):
            idle_pass(xq, zeros)
        quantize(xq, 256, N)
        interleave(vcopy, wq, 0, w_raw, 0, 48)
        interleave(scopy, wq, 48, w_raw, 48, 80)
        interleave(scopy, wq, 128, w_raw, 128, 128)
        quantize(wq, 0, T)
        products(0, wq, xq, 0)
        interleave(vcopy, uq, 0, u0_raw, 0, T)
        quantize(wq, T, M)
        quantize(uq, 0, T)
        products(1, uq, xq, 0)
        products(2, wq, xq, T)
        interleave(vcopy, uq, T, u1_raw, 0, T)
        gelu(0, 0)
        quantize(uq, T, M)
        products(3, uq, xq, T)
        gate(0, 0)
        gelu(1, 0)
        gate(1, 0)
        gelu(0, 1)
        gate(0, 1)
        gelu(1, 1)
        gate(1, 1)
